import numpy as np
import ml_dtypes


def mxq(x, axis, fmt="e4m3"):
    dtype, down = {"e4m3": (ml_dtypes.float8_e4m3fn, 7), "e5m2": (ml_dtypes.float8_e5m2, 14)}[fmt]
    v = np.moveaxis(np.asarray(x, np.float32).astype(ml_dtypes.bfloat16).astype(np.float64), axis, -1)
    blocks = v.reshape(v.shape[:-1] + (-1, 32))
    amax = np.abs(blocks).max(-1, keepdims=True)
    byte = np.maximum(np.where(amax > 0, np.frexp(amax)[1] - 1 + 127, 0) - down, 1)
    scale = np.exp2(byte - 127.0)
    codes = (blocks / scale).astype(np.float32).astype(dtype).astype(np.float64)
    return np.moveaxis((codes * scale).reshape(v.shape), -1, axis)


WIDE = False


def mx_kscale(k):
    if not WIDE:
        return np.ones(k)
    levels = np.array([10, -10, 5, -5, 0])
    if k % 512:
        return np.exp2(np.random.permutation(np.resize(levels, k // 32))).repeat(32)
    a = np.empty((k // 512, 16))
    for p in range(k // 512):
        a[p, :8] = np.random.permutation(np.resize(levels, 8))
        for g in range(8):
            far = levels[np.abs(levels - a[p, g]) >= 10]
            a[p, g + 8] = far[np.random.randint(len(far))]
    return np.exp2(a.ravel()).repeat(32)


BF16 = ml_dtypes.bfloat16


def bf(x):
    return np.asarray(x, np.float32).astype(BF16)


def f64(x):
    return np.asarray(x).astype(np.float64)


N, D, F = 2048, 512, 1024


def draw0():
    s, t = mx_kscale(D), mx_kscale(N)
    x = np.random.standard_normal((N, D)) * s[None, :]
    f = np.random.standard_normal((N, D)) * s[None, :] / t[:, None]
    w = np.random.standard_normal((D, F)) / np.sqrt(D) / s[:, None]
    b = 0.5 * np.random.standard_normal(F)
    q = (1.0 + 0.1 * np.random.standard_normal(N)) * t
    return {"x": bf(x), "f": bf(f), "w": bf(w), "b": bf(b), "q": bf(q)}


def core(x, f, w, b, q):
    n_samples = x.shape[0]
    wq = mxq(f64(w), 0, "e4m3")
    psi = np.tanh((mxq(f64(x), 1, "e4m3") @ wq) + f64(b)[None, :])
    zd = mxq(f64(f), 1, "e4m3") @ wq
    lpsi = (1.0 - psi * psi) * zd
    a = f64(q)[:, None] * psi
    return (mxq(a, 0, "e4m3").T @ mxq(lpsi, 0, "e4m3")) / np.sqrt(n_samples)


def e4m3fn_bytes(y):
    return np.clip(np.asarray(y, np.float64), -448.0, 448.0).astype(np.float32).astype(ml_dtypes.float8_e4m3fn).view(np.uint8)


def e4m3fn_values(b):
    return np.asarray(b, np.uint8).view(ml_dtypes.float8_e4m3fn).astype(np.float64)


def setup_inputs():
    d = draw0()
    x0 = np.asarray(d['x']).astype(np.float64)
    s = (np.max(np.abs(x0), axis=(0,), keepdims=True) / 448.0).astype(np.float32)
    out = {}
    for k, v in d.items():
        if k == 'x':
            out['x_bytes'] = e4m3fn_bytes(x0 / s.astype(np.float64))
            out['x_scale'] = s
        else:
            out[k] = v
    return out


def reference(x_bytes, x_scale, f, w, b, q):
    return core(e4m3fn_values(x_bytes) * x_scale.astype(np.float64), f, w, b, q)

@@ -1,0 +1,415 @@
+import math
+from contextlib import ExitStack
+
+import concourse.mybir as mybir
+from concourse.masks import make_identity
+
+N, D, F = 2048, 512, 1024
+FLOPS = 2 * N * D * F * 2 + 2 * N * F * F
+
+F32 = mybir.dt.float32
+BF16 = mybir.dt.bfloat16
+U32 = mybir.dt.uint32
+U8 = mybir.dt.uint8
+FP8 = mybir.dt.float8_e4m3fn
+FP8X4 = mybir.dt.float8_e4m3fn_x4
+ADD = mybir.AluOpType.add
+MULT = mybir.AluOpType.mult
+COPY = mybir.ActivationFunctionType.Copy
+TANH = mybir.ActivationFunctionType.Tanh
+SQUARE = mybir.ActivationFunctionType.Square
+
+P = 128
+T4 = 4
+GROUP = P * T4
+GROUPS = N // GROUP
+CHUNKS = F // P
+TURNED = 4
+OUT_SCALE = -1.0 / math.sqrt(N)
+PAIRS = [(0, 0), (1, 0), (0, 1), (1, 1)] + [(c, h) for c in range(2, CHUNKS) for h in range(2)]
+
+
+def tile_generatoredmdstiffnessmatrix_kernel(tc, x_bytes, x_scale, f, w, b, q, out):
+    nc = tc.nc
+    with ExitStack() as ctx:
+        keep = ctx.enter_context(tc.tile_pool(name="keep", bufs=1))
+        stage = ctx.enter_context(tc.tile_pool(name="stage", bufs=2))
+        psum = ctx.enter_context(tc.psum_pool(name="psum", bufs=2))
+        ctx.enter_context(tc.manual_schedule())
+
+        scale_rows = keep.tile([P, P], F32)
+        nc.vector.memset(scale_rows[:], 0.0)
+        warm = keep.tile([P, 1], F32)
+        nc.vector.memset(warm[:], 0.0)
+        ident = keep.tile([P, P], F32)
+        make_identity(nc, ident[:])
+        bias_rows = keep.tile([P, P], F32)
+        nc.gpsimd.memset(bias_rows[:], 0.0)
+
+        nc.sync.dma_start(out=scale_rows[0:4, :], in_=x_scale.rearrange("o (c n) -> (o c) n", n=P))
+        b_rows = keep.tile([CHUNKS, P], BF16)
+        nc.scalar.dma_start(out=b_rows[:], in_=b.rearrange("(c m) -> c m", m=P))
+        warm_out = keep.tile([P, 1], F32)
+        nc.scalar.activation(out=warm_out[:], in_=warm[:], func=TANH)
+
+        w_view = w.rearrange("(p j) c -> p j c", j=T4)
+        w_raw = [keep.tile([P, T4, 512], BF16, name="w_raw%d" % i) for i in range(2)]
+        f_raw = [keep.tile([P, T4, D], BF16, name="f_raw%d" % g) for g in range(GROUPS)]
+        x_raw = [keep.tile([P, T4 * D], U8, name="x_raw%d" % g) for g in range(GROUPS)]
+        f_view = f.rearrange("(g p t) k -> g p t k", p=P, t=T4)
+        x_view = x_bytes.rearrange("(g p t) k -> g p (t k)", p=P, t=T4)
+
+        def load_w(i):
+            nc.sync.dma_start(out=w_raw[i][:], in_=w_view[:, :, 512 * i:512 * (i + 1)])
+
+        def load_f(g):
+            nc.sync.dma_start(out=f_raw[g][:], in_=f_view[g])
+
+        def load_x(g):
+            nc.sync.dma_start(out=x_raw[g][:], in_=x_view[g])
+
+        q_all = keep.tile([P, GROUPS, T4], BF16)
+        b_all = keep.tile([P, F], BF16)
+        load_w(0)
+        load_f(0)
+        load_x(0)
+        load_x(1)
+        load_f(1)
+        nc.sync.dma_start(out=q_all[:], in_=q.rearrange("(g p t) -> p g t", p=P, t=T4))
+        load_x(2)
+        load_x(3)
+        load_f(2)
+        load_f(3)
+        load_w(1)
+        nc.sync.dma_start(out=b_all[:], in_=b.partition_broadcast(P))
+
+        s_turn = psum.tile([P, P], F32, tag="zt", name="s_turn")
+        nc.tensor.transpose(s_turn[:], scale_rows[:], ident[:])
+        s_cols = keep.tile([P, T4], F32)
+        nc.scalar.copy(out=s_cols[:], in_=s_turn[:, 0:4])
+        s_bank = psum.tile([P, D], F32, tag="zt", name="s_bank")
+        for c in range(4):
+            nc.tensor.transpose(s_bank[:, P * c:P * (c + 1)], s_cols[:, c:c + 1].to_broadcast([P, P]), ident[:])
+        s_all = keep.tile([P, D], F32)
+        nc.scalar.copy(out=s_all[:], in_=s_bank[:])
+
+        w_codes = [keep.tile([P, 512], U32, align_bytes=64, name="w_codes%d" % i) for i in range(2)]
+        w_scales = [keep.tile([P, 512], U8, align_bytes=64, name="w_scales%d" % i) for i in range(2)]
+        x_codes = [keep.tile([P, GROUP], U32, align_bytes=64, name="x_codes%d" % g) for g in range(GROUPS)]
+        x_scales = [keep.tile([P, GROUP], U8, align_bytes=64, name="x_scales%d" % g) for g in range(GROUPS)]
+        f_codes = [keep.tile([P, GROUP], U32, align_bytes=64, name="f_codes%d" % g) for g in range(GROUPS)]
+        f_scales = [keep.tile([P, GROUP], U8, align_bytes=64, name="f_scales%d" % g) for g in range(GROUPS)]
+        a_codes = keep.tile([P, CHUNKS, GROUPS, P], U32, align_bytes=64)
+        a_scales = keep.tile([P, CHUNKS, GROUPS, P], U8, align_bytes=64)
+        l_codes = [keep.tile([P, F], U32, align_bytes=64, name="l_codes%d" % g) for g in range(GROUPS)]
+        l_scales = [keep.tile([P, F], U8, align_bytes=64, name="l_scales%d" % g) for g in range(GROUPS)]
+
+        def quantize(codes, scales, values):
+            nc.vector.quantize_mx(out=codes.bitcast(FP8X4), scales=scales, in_=values)
+
+        w_mx = [keep.tile([P, 512 * T4], BF16, align_bytes=64, name="w_mx%d" % i) for i in range(2)]
+
+        def interleave_w(engine_copy, i):
+            engine_copy(out=w_mx[i][:].rearrange("p (c j) -> p c j", j=T4), in_=w_raw[i][:].rearrange("p j c -> p c j"))
+
+        def quantize_w(i):
+            quantize(w_codes[i][:], w_scales[i][:], w_mx[i][:])
+
+        x_vals = {}
+        mx_in = {}
+
+        def widen(g, t):
+            if t == 0:
+                x_vals[g] = stage.tile([P, T4 * D], BF16, tag="x_val", bufs=3, name="x_val%d" % g)
+            cols = slice(D * t, D * (t + 1))
+            nc.vector.tensor_tensor(out=x_vals[g][:, cols], in0=x_raw[g][:, cols].bitcast(FP8), in1=s_all[:], op=MULT)
+
+        turn_tags = ["ps", "out", "zd"]
+        turned = [0]
+
+        def turn(kind, g, half):
+            if half == 0:
+                mx_in[kind, g] = stage.tile([P, GROUP * T4], BF16, tag="mx_in", bufs=4, align_bytes=64, name="mx_in_%s%d" % (kind, g))
+            src = x_vals[g][:] if kind == "x" else f_raw[g][:].rearrange("p t k -> p (t k)")
+            words = src.bitcast(F32)
+            bank = psum.tile([P, 2, 2, P], F32, tag=turn_tags[turned[0] % len(turn_tags)], name="turn")
+            turned[0] += 1
+            for s in range(2):
+                w0 = 256 * (2 * half + s)
+                for u in range(2):
+                    nc.tensor.transpose(bank[:, s, u, :], words[:, w0 + u:w0 + 256:2], ident[:])
+            dst = mx_in[kind, g][:].bitcast(F32)[:, 512 * half:512 * (half + 1)]
+            nc.scalar.copy(out=dst.rearrange("p (s r u) -> p s r u", s=2, u=2), in_=bank[:].rearrange("p s u r -> p s r u"))
+
+        def quantize_rows(kind, g):
+            if kind == "x":
+                quantize(x_codes[g][:], x_scales[g][:], mx_in[kind, g][:])
+            else:
+                quantize(f_codes[g][:], f_scales[g][:], mx_in[kind, g][:])
+
+        def w_cols(c):
+            cols = slice(P * (c % 4), P * (c % 4 + 1))
+            return w_codes[c // 4][:, cols].bitcast(FP8X4), w_scales[c // 4][:, cols]
+
+        live = {}
+
+        def groups(k):
+            c, h = PAIRS[k]
+            return [2 * h, 2 * h + 1]
+
+        def is_turned(k):
+            return 0 <= k < len(PAIRS) and PAIRS[k][0] < TURNED
+
+        def is_direct(k):
+            return 0 <= k < len(PAIRS) and PAIRS[k][0] >= TURNED
+
+        def sample_first(codes, scales, g, c, tag, name):
+            bank = psum.tile([P, T4, P], F32, tag=tag, name=name)
+            rhs, rhs_scale = w_cols(c)
+            for t in range(T4):
+                cols = slice(P * t, P * (t + 1))
+                nc.tensor.matmul_mx(out=bank[:, t, :], lhsT=codes[g][:, cols].bitcast(FP8X4), lhsT_scale=scales[g][:, cols],
+                                    rhs=rhs, rhs_scale=rhs_scale, start=True, stop=True)
+            return bank
+
+        def z_step(k):
+            c = PAIRS[k][0]
+            banks = []
+            for g in groups(k):
+                if is_turned(k):
+                    bank = psum.tile([P, GROUP], F32, tag="zt", name="zt")
+                    lhs, lhs_scale = w_cols(c)
+                    nc.tensor.matmul_mx(out=bank[:], lhsT=lhs, lhsT_scale=lhs_scale, rhs=x_codes[g][:].bitcast(FP8X4),
+                                        rhs_scale=x_scales[g][:], start=True, stop=True)
+                else:
+                    bank = sample_first(x_codes, x_scales, g, c, "zt", "z")
+                banks.append(bank)
+            live["z", k] = banks
+
+        def bias_step(k):
+            c = PAIRS[k][0]
+            zb = stage.tile([P, 2, P, T4], F32, tag="zb", bufs=2, name="zb")
+            bias = b_all[:, P * c:P * (c + 1)].unsqueeze(2).to_broadcast([P, P, T4])
+            for i in range(2):
+                nc.vector.tensor_tensor(out=zb[:, i], in0=live["z", k][i][:].rearrange("p t n -> p n t"), in1=bias, op=ADD)
+            live["zb", k] = zb
+
+        def tanh_step(k):
+            c = PAIRS[k][0]
+            psi = stage.tile([P, 2, GROUP], F32, tag="psi", bufs=3, name="psi")
+            for i in range(2):
+                if is_turned(k):
+                    nc.scalar.activation(out=psi[:, i], in_=live["z", k][i][:], func=TANH, bias=b_cols[:, c:c + 1])
+                else:
+                    nc.scalar.activation(out=psi[:, i], in_=live["zb", k][:, i].rearrange("p n t -> p (n t)"), func=TANH)
+            live["psi", k] = psi
+
+        def turn_psi_step(k):
+            banks = []
+            for i in range(2):
+                bank = psum.tile([P, T4, P], F32, tag="ps", name="ps")
+                for t in range(T4):
+                    nc.tensor.transpose(bank[:, t, :], live["psi", k][:, i, P * t:P * (t + 1)], ident[:])
+                banks.append(bank)
+            live["ps", k] = banks
+
+        def square_step(k):
+            sq = stage.tile([P, 2, P, T4], F32, tag="sq", bufs=2, name="sq")
+            for i in range(2):
+                if is_turned(k):
+                    nc.scalar.activation(out=sq[:, i], in_=live["ps", k][i][:].rearrange("p t n -> p n t"), func=SQUARE)
+                else:
+                    nc.scalar.activation(out=sq[:, i].rearrange("p n t -> p (n t)"), in_=live["psi", k][:, i], func=SQUARE)
+            live["sq", k] = sq
+
+        def a_step(k):
+            a_mx = stage.tile([P, 2, P, T4], BF16, tag="a_mx", bufs=3, align_bytes=64, name="a_mx")
+            for i, g in enumerate(groups(k)):
+                weight = q_all[:, g, :].unsqueeze(1).to_broadcast([P, P, T4])
+                if is_turned(k):
+                    nc.vector.tensor_tensor(out=a_mx[:, i], in0=live["ps", k][i][:].rearrange("p t n -> p n t"), in1=weight, op=MULT)
+                else:
+                    nc.gpsimd.tensor_tensor(out=a_mx[:, i], in0=live["psi", k][:, i].rearrange("p (n t) -> p n t", t=T4), in1=weight, op=MULT)
+            live["a", k] = a_mx
+
+        def zd_step(k):
+            live["zd", k] = [sample_first(f_codes, f_scales, g, PAIRS[k][0], "zd", "zd") for g in groups(k)]
+
+        def l_step(k):
+            l_mx = stage.tile([P, 2, P, T4], BF16, tag="l_mx", bufs=3, align_bytes=64, name="l_mx")
+            for i in range(2):
+                nc.vector.scalar_tensor_tensor(out=l_mx[:, i], in0=live["sq", k][:, i], scalar=-1.0,
+                                               in1=live["zd", k][i][:].rearrange("p t n -> p n t"), op0=ADD, op1=MULT)
+            live["l", k] = l_mx
+
+        def quantize_a(k):
+            c, h = PAIRS[k]
+            quantize(a_codes[:, c, 2 * h:2 * h + 2, :].rearrange("p g n -> p (g n)"),
+                     a_scales[:, c, 2 * h:2 * h + 2, :].rearrange("p g n -> p (g n)"),
+                     live["a", k][:].rearrange("p i n t -> p (i n t)"))
+
+        def quantize_l(k):
+            c = PAIRS[k][0]
+            cols = slice(P * c, P * (c + 1))
+            for i, g in enumerate(groups(k)):
+                quantize(l_codes[g][:, cols], l_scales[g][:, cols], live["l", k][:, i].rearrange("p n t -> p (n t)"))
+
+        out_rows = out.rearrange("(i p) n -> p i n", p=P)
+        ready = []
+        copies = []
+
+        def add_blocks(c):
+            blocks = [(c, j) for j in range(c + 1)] + [(i, c) for i in range(c)]
+            for s in range(0, len(blocks), 4):
+                ready.append((c, blocks[s:s + 4]))
+
+        def out_step():
+            c, blocks = ready.pop(0)
+            width = P * len(blocks)
+            bank = psum.tile([P, 512], F32, tag="out", name="acc")
+            row = [j for i, j in blocks if i == c]
+            col = [i for i, j in blocks if i != c]
+            runs = []
+            at = 0
+            while row:
+                n = 4 if len(row) == 4 else 2 if len(row) >= 2 else 1
+                runs.append((c, row[0], n, at))
+                row = row[n:]
+                at += n
+            for i in col:
+                runs.append((i, c, 1, at))
+                at += 1
+            for i, j, n, pos in runs:
+                cols = slice(P * j, P * (j + n))
+                for g in range(GROUPS):
+                    nc.tensor.matmul_mx(out=bank[:, P * pos:P * (pos + n)], lhsT=a_codes[:, i, g, :].bitcast(FP8X4), lhsT_scale=a_scales[:, i, g, :],
+                                        rhs=l_codes[g][:, cols].bitcast(FP8X4), rhs_scale=l_scales[g][:, cols],
+                                        start=(g == 0), stop=(g == GROUPS - 1))
+            copies.append((c, blocks, bank, width))
+
+        def copy_out(engine):
+            c, blocks, bank, width = copies.pop(0)
+            res = stage.tile([P, 512], F32, tag="res", bufs=4, name="res")
+            if engine == "scalar":
+                nc.scalar.activation(out=res[:, :width], in_=bank[:, :width], func=COPY, scale=OUT_SCALE)
+            else:
+                nc.vector.tensor_scalar(out=res[:, :width], in0=bank[:, :width], scalar1=OUT_SCALE, scalar2=None, op0=MULT)
+            row = [j for i, j in blocks if i == c]
+            col = [i for i, j in blocks if i != c]
+            if row:
+                nc.sync.dma_start(out=out[P * c:P * (c + 1), P * row[0]:P * (row[-1] + 1)], in_=res[:, :P * len(row)])
+            if col:
+                nc.sync.dma_start(out=out_rows[:, col[0]:col[-1] + 1, P * c:P * (c + 1)],
+                                  in_=res[:, P * len(row):width].rearrange("p (i n) -> p i n", n=P))
+
+        interleave_w(nc.vector.tensor_copy, 0)
+        turn("f", 0, 0)
+        turn("f", 0, 1)
+        nc.scalar.copy(out=bias_rows[0:CHUNKS, :], in_=b_rows[:])
+        b_turn = psum.tile([P, P], F32, tag="zt", name="b_turn")
+        nc.tensor.transpose(b_turn[:], bias_rows[:], ident[:])
+        b_cols = keep.tile([P, CHUNKS], F32)
+        nc.scalar.copy(out=b_cols[:], in_=b_turn[:, 0:CHUNKS])
+        widen(0, 0)
+        widen(0, 1)
+        turn("x", 0, 0)
+        quantize_w(0)
+        widen(0, 2)
+        widen(0, 3)
+        turn("x", 0, 1)
+        quantize_rows("f", 0)
+        widen(1, 0)
+        widen(1, 1)
+        turn("x", 1, 0)
+        quantize_rows("x", 0)
+        widen(1, 2)
+        widen(1, 3)
+        turn("x", 1, 1)
+        turn("f", 1, 0)
+        turn("f", 1, 1)
+        widen(2, 0)
+        quantize_rows("x", 1)
+        widen(2, 1)
+        quantize_rows("f", 1)
+        z_step(0)
+        tanh_step(0)
+        z_step(1)
+        tanh_step(1)
+
+        turn_tags.remove("zd")
+        turned[0] = 0
+
+        def extra_0():
+            turn("x", 2, 0)
+            widen(2, 2)
+            widen(2, 3)
+            turn("x", 2, 1)
+            widen(3, 0)
+            widen(3, 1)
+            turn("x", 3, 0)
+            quantize_rows("x", 2)
+            widen(3, 2)
+            widen(3, 3)
+            turn("x", 3, 1)
+
+        def extra_1():
+            turn("f", 2, 0)
+            turn("f", 2, 1)
+            turn("f", 3, 0)
+            quantize_rows("f", 2)
+            turn("f", 3, 1)
+            quantize_rows("f", 3)
+
+        last = len(PAIRS) - 1
+        for k in range(len(PAIRS)):
+            if is_turned(k):
+                turn_psi_step(k)
+                square_step(k)
+                a_step(k)
+            if k == 0:
+                zd_step(0)
+                extra_0()
+                quantize_rows("x", 3)
+                z_step(2)
+            elif k + 2 <= last:
+                z_step(k + 2)
+            if is_turned(k) and k > 0:
+                zd_step(k)
+            if is_turned(k + 2):
+                tanh_step(k + 2)
+            if is_turned(k) and k > 0:
+                quantize_l(k - 1)
+            l_step(k)
+            if is_direct(k):
+                quantize_l(k - 1)
+            if is_direct(k + 2):
+                bias_step(k + 2)
+            if is_direct(k + 1):
+                zd_step(k + 1)
+                tanh_step(k + 1)
+                square_step(k + 1)
+                a_step(k + 1)
+            quantize_a(k)
+            if k == 0:
+                extra_1()
+                interleave_w(nc.scalar.copy, 1)
+            if k == 1:
+                quantize_w(1)
+            if k > 0:
+                cp, hp = PAIRS[k - 1]
+                if hp == 1:
+                    add_blocks(cp)
+            for turn_out in range(2 if k < last else 0):
+                if ready:
+                    out_step()
+                    copy_out("scalar")
+        quantize_l(last)
+        while ready:
+            out_step()
+            copy_out("scalar")
+        add_blocks(CHUNKS - 1)
+        order = 0
+        while ready:
+            out_step()
+            copy_out("scalar" if order % 2 else "vector")
+            order += 1

@@ -23,10 +23,12 @@ P = 128
 T4 = 4
 GROUP = P * T4
 GROUPS = N // GROUP
+WQ = 256
+SINGLE = 6
 CHUNKS = F // P
-TURNED = 4
 OUT_SCALE = -1.0 / math.sqrt(N)
 PAIRS = [(0, 0), (1, 0), (0, 1), (1, 1)] + [(c, h) for c in range(2, CHUNKS) for h in range(2)]
+MODES = "TTTTTTTT"
 
 
 def tile_generatoredmdstiffnessmatrix_kernel(tc, x_bytes, x_scale, f, w, b, q, out):
@@ -35,7 +37,6 @@ def tile_generatoredmdstiffnessmatrix_kernel(tc, x_bytes, x_scale, f, w, b, q, o
         keep = ctx.enter_context(tc.tile_pool(name="keep", bufs=1))
         stage = ctx.enter_context(tc.tile_pool(name="stage", bufs=2))
         psum = ctx.enter_context(tc.psum_pool(name="psum", bufs=2))
-        ctx.enter_context(tc.manual_schedule())
 
         scale_rows = keep.tile([P, P], F32)
         nc.vector.memset(scale_rows[:], 0.0)
@@ -53,14 +54,14 @@ def tile_generatoredmdstiffnessmatrix_kernel(tc, x_bytes, x_scale, f, w, b, q, o
         nc.scalar.activation(out=warm_out[:], in_=warm[:], func=TANH)
 
         w_view = w.rearrange("(p j) c -> p j c", j=T4)
-        w_raw = [keep.tile([P, T4, 512], BF16, name="w_raw%d" % i) for i in range(2)]
+        w_raw = [keep.tile([P, T4, WQ], BF16, name="w_raw%d" % i) for i in range(F // WQ)]
         f_raw = [keep.tile([P, T4, D], BF16, name="f_raw%d" % g) for g in range(GROUPS)]
         x_raw = [keep.tile([P, T4 * D], U8, name="x_raw%d" % g) for g in range(GROUPS)]
         f_view = f.rearrange("(g p t) k -> g p t k", p=P, t=T4)
         x_view = x_bytes.rearrange("(g p t) k -> g p (t k)", p=P, t=T4)
 
         def load_w(i):
-            nc.sync.dma_start(out=w_raw[i][:], in_=w_view[:, :, 512 * i:512 * (i + 1)])
+            nc.sync.dma_start(out=w_raw[i][:], in_=w_view[:, :, WQ * i:WQ * (i + 1)])
 
         def load_f(g):
             nc.sync.dma_start(out=f_raw[g][:], in_=f_view[g])
@@ -69,19 +70,19 @@ def tile_generatoredmdstiffnessmatrix_kernel(tc, x_bytes, x_scale, f, w, b, q, o
             nc.sync.dma_start(out=x_raw[g][:], in_=x_view[g])
 
         q_all = keep.tile([P, GROUPS, T4], BF16)
-        b_all = keep.tile([P, F], BF16)
         load_w(0)
-        load_f(0)
         load_x(0)
+        load_f(0)
         load_x(1)
-        load_f(1)
         nc.sync.dma_start(out=q_all[:], in_=q.rearrange("(g p t) -> p g t", p=P, t=T4))
+        load_f(1)
         load_x(2)
+        load_w(1)
         load_x(3)
         load_f(2)
         load_f(3)
-        load_w(1)
-        nc.sync.dma_start(out=b_all[:], in_=b.partition_broadcast(P))
+        load_w(2)
+        load_w(3)
 
         s_turn = psum.tile([P, P], F32, tag="zt", name="s_turn")
         nc.tensor.transpose(s_turn[:], scale_rows[:], ident[:])
@@ -90,11 +91,12 @@ def tile_generatoredmdstiffnessmatrix_kernel(tc, x_bytes, x_scale, f, w, b, q, o
         s_bank = psum.tile([P, D], F32, tag="zt", name="s_bank")
         for c in range(4):
             nc.tensor.transpose(s_bank[:, P * c:P * (c + 1)], s_cols[:, c:c + 1].to_broadcast([P, P]), ident[:])
-        s_all = keep.tile([P, D], F32)
-        nc.scalar.copy(out=s_all[:], in_=s_bank[:])
+        s_all = keep.tile([P, 2, D], F32)
+        for i in range(2):
+            nc.scalar.copy(out=s_all[:, i, :], in_=s_bank[:])
 
-        w_codes = [keep.tile([P, 512], U32, align_bytes=64, name="w_codes%d" % i) for i in range(2)]
-        w_scales = [keep.tile([P, 512], U8, align_bytes=64, name="w_scales%d" % i) for i in range(2)]
+        w_codes = keep.tile([P, F], U32, align_bytes=64)
+        w_scales = keep.tile([P, F], U8, align_bytes=64)
         x_codes = [keep.tile([P, GROUP], U32, align_bytes=64, name="x_codes%d" % g) for g in range(GROUPS)]
         x_scales = [keep.tile([P, GROUP], U8, align_bytes=64, name="x_scales%d" % g) for g in range(GROUPS)]
         f_codes = [keep.tile([P, GROUP], U32, align_bytes=64, name="f_codes%d" % g) for g in range(GROUPS)]
@@ -107,22 +109,22 @@ def tile_generatoredmdstiffnessmatrix_kernel(tc, x_bytes, x_scale, f, w, b, q, o
         def quantize(codes, scales, values):
             nc.vector.quantize_mx(out=codes.bitcast(FP8X4), scales=scales, in_=values)
 
-        w_mx = [keep.tile([P, 512 * T4], BF16, align_bytes=64, name="w_mx%d" % i) for i in range(2)]
+        w_mx = [keep.tile([P, WQ * T4], BF16, align_bytes=64, name="w_mx%d" % i) for i in range(F // WQ)]
 
         def interleave_w(engine_copy, i):
             engine_copy(out=w_mx[i][:].rearrange("p (c j) -> p c j", j=T4), in_=w_raw[i][:].rearrange("p j c -> p c j"))
 
         def quantize_w(i):
-            quantize(w_codes[i][:], w_scales[i][:], w_mx[i][:])
+            quantize(w_codes[:, WQ * i:WQ * (i + 1)], w_scales[:, WQ * i:WQ * (i + 1)], w_mx[i][:])
 
         x_vals = {}
         mx_in = {}
 
-        def widen(g, t):
-            if t == 0:
+        def widen(g, half):
+            if half == 0:
                 x_vals[g] = stage.tile([P, T4 * D], BF16, tag="x_val", bufs=3, name="x_val%d" % g)
-            cols = slice(D * t, D * (t + 1))
-            nc.vector.tensor_tensor(out=x_vals[g][:, cols], in0=x_raw[g][:, cols].bitcast(FP8), in1=s_all[:], op=MULT)
+            cols = slice(2 * D * half, 2 * D * (half + 1))
+            nc.vector.tensor_tensor(out=x_vals[g][:, cols], in0=x_raw[g][:, cols].bitcast(FP8), in1=s_all[:].rearrange("p i k -> p (i k)"), op=MULT)
 
         turn_tags = ["ps", "out", "zd"]
         turned = [0]
@@ -148,8 +150,8 @@ def tile_generatoredmdstiffnessmatrix_kernel(tc, x_bytes, x_scale, f, w, b, q, o
                 quantize(f_codes[g][:], f_scales[g][:], mx_in[kind, g][:])
 
         def w_cols(c):
-            cols = slice(P * (c % 4), P * (c % 4 + 1))
-            return w_codes[c // 4][:, cols].bitcast(FP8X4), w_scales[c // 4][:, cols]
+            cols = slice(P * c, P * (c + 1))
+            return w_codes[:, cols].bitcast(FP8X4), w_scales[:, cols]
 
         live = {}
 
@@ -158,10 +160,10 @@ def tile_generatoredmdstiffnessmatrix_kernel(tc, x_bytes, x_scale, f, w, b, q, o
             return [2 * h, 2 * h + 1]
 
         def is_turned(k):
-            return 0 <= k < len(PAIRS) and PAIRS[k][0] < TURNED
+            return 0 <= k < len(PAIRS) and MODES[PAIRS[k][0]] == "T"
 
         def is_direct(k):
-            return 0 <= k < len(PAIRS) and PAIRS[k][0] >= TURNED
+            return 0 <= k < len(PAIRS) and MODES[PAIRS[k][0]] != "T"
 
         def sample_first(codes, scales, g, c, tag, name):
             bank = psum.tile([P, T4, P], F32, tag=tag, name=name)
@@ -186,17 +188,9 @@ def tile_generatoredmdstiffnessmatrix_kernel(tc, x_bytes, x_scale, f, w, b, q, o
                 banks.append(bank)
             live["z", k] = banks
 
-        def bias_step(k):
-            c = PAIRS[k][0]
-            zb = stage.tile([P, 2, P, T4], F32, tag="zb", bufs=2, name="zb")
-            bias = b_all[:, P * c:P * (c + 1)].unsqueeze(2).to_broadcast([P, P, T4])
-            for i in range(2):
-                nc.vector.tensor_tensor(out=zb[:, i], in0=live["z", k][i][:].rearrange("p t n -> p n t"), in1=bias, op=ADD)
-            live["zb", k] = zb
-
         def tanh_step(k):
             c = PAIRS[k][0]
-            psi = stage.tile([P, 2, GROUP], F32, tag="psi", bufs=3, name="psi")
+            psi = stage.tile([P, 2, GROUP], F32, tag="psi", bufs=4, name="psi")
             for i in range(2):
                 if is_turned(k):
                     nc.scalar.activation(out=psi[:, i], in_=live["z", k][i][:], func=TANH, bias=b_cols[:, c:c + 1])
@@ -214,7 +208,7 @@ def tile_generatoredmdstiffnessmatrix_kernel(tc, x_bytes, x_scale, f, w, b, q, o
             live["ps", k] = banks
 
         def square_step(k):
-            sq = stage.tile([P, 2, P, T4], F32, tag="sq", bufs=2, name="sq")
+            sq = stage.tile([P, 2, P, T4], F32, tag="sq", bufs=4, name="sq")
             for i in range(2):
                 if is_turned(k):
                     nc.scalar.activation(out=sq[:, i], in_=live["ps", k][i][:].rearrange("p t n -> p n t"), func=SQUARE)
@@ -223,193 +217,198 @@ def tile_generatoredmdstiffnessmatrix_kernel(tc, x_bytes, x_scale, f, w, b, q, o
             live["sq", k] = sq
 
         def a_step(k):
-            a_mx = stage.tile([P, 2, P, T4], BF16, tag="a_mx", bufs=3, align_bytes=64, name="a_mx")
+            c, h = PAIRS[k]
+            if h == 0:
+                live["a", c] = stage.tile([P, GROUPS, P, T4], BF16, tag="a_mx", bufs=3, align_bytes=64, name="a_mx")
+            a_mx = live["a", c]
             for i, g in enumerate(groups(k)):
                 weight = q_all[:, g, :].unsqueeze(1).to_broadcast([P, P, T4])
                 if is_turned(k):
-                    nc.vector.tensor_tensor(out=a_mx[:, i], in0=live["ps", k][i][:].rearrange("p t n -> p n t"), in1=weight, op=MULT)
+                    nc.vector.tensor_tensor(out=a_mx[:, g], in0=live["ps", k][i][:].rearrange("p t n -> p n t"), in1=weight, op=MULT)
+                elif MODES[PAIRS[k][0]] == "V" or (MODES[PAIRS[k][0]] == "H" and i == 1):
+                    nc.vector.tensor_tensor(out=a_mx[:, g], in0=live["psi", k][:, i].rearrange("p (n t) -> p n t", t=T4), in1=weight, op=MULT)
                 else:
-                    nc.gpsimd.tensor_tensor(out=a_mx[:, i], in0=live["psi", k][:, i].rearrange("p (n t) -> p n t", t=T4), in1=weight, op=MULT)
-            live["a", k] = a_mx
+                    nc.gpsimd.tensor_tensor(out=a_mx[:, g], in0=live["psi", k][:, i].rearrange("p (n t) -> p n t", t=T4), in1=weight, op=MULT)
 
         def zd_step(k):
             live["zd", k] = [sample_first(f_codes, f_scales, g, PAIRS[k][0], "zd", "zd") for g in groups(k)]
 
         def l_step(k):
-            l_mx = stage.tile([P, 2, P, T4], BF16, tag="l_mx", bufs=3, align_bytes=64, name="l_mx")
-            for i in range(2):
-                nc.vector.scalar_tensor_tensor(out=l_mx[:, i], in0=live["sq", k][:, i], scalar=-1.0,
-                                               in1=live["zd", k][i][:].rearrange("p t n -> p n t"), op0=ADD, op1=MULT)
-            live["l", k] = l_mx
-
-        def quantize_a(k):
             c, h = PAIRS[k]
-            quantize(a_codes[:, c, 2 * h:2 * h + 2, :].rearrange("p g n -> p (g n)"),
-                     a_scales[:, c, 2 * h:2 * h + 2, :].rearrange("p g n -> p (g n)"),
-                     live["a", k][:].rearrange("p i n t -> p (i n t)"))
-
-        def quantize_l(k):
-            c = PAIRS[k][0]
-            cols = slice(P * c, P * (c + 1))
+            if h == 0 and (c % 2 == 0 or c >= SINGLE):
+                live["l", c] = stage.tile([P, GROUPS, 2, P, T4], BF16, tag="l_mx", bufs=2, align_bytes=64, name="l_mx")
+                if c < SINGLE:
+                    live["l", c + 1] = live["l", c]
+            at = 0 if c >= SINGLE else c % 2
             for i, g in enumerate(groups(k)):
-                quantize(l_codes[g][:, cols], l_scales[g][:, cols], live["l", k][:, i].rearrange("p n t -> p (n t)"))
+                nc.vector.scalar_tensor_tensor(out=live["l", c][:, g, at], in0=live["sq", k][:, i], scalar=-1.0,
+                                               in1=live["zd", k][i][:].rearrange("p t n -> p n t"), op0=ADD, op1=MULT)
+
+        def quantize_a(c, gs):
+            quantize(a_codes[:, c, gs, :].rearrange("p g n -> p (g n)"), a_scales[:, c, gs, :].rearrange("p g n -> p (g n)"),
+                     live["a", c][:, gs].rearrange("p g n t -> p (g n t)"))
+
+        def quantize_l(c, width, g):
+            cols = slice(P * c, P * (c + width))
+            quantize(l_codes[g][:, cols], l_scales[g][:, cols], live["l", c][:, g, 0:width].rearrange("p c n t -> p (c n t)"))
 
         out_rows = out.rearrange("(i p) n -> p i n", p=P)
         ready = []
-        copies = []
 
-        def add_blocks(c):
-            blocks = [(c, j) for j in range(c + 1)] + [(i, c) for i in range(c)]
-            for s in range(0, len(blocks), 4):
-                ready.append((c, blocks[s:s + 4]))
+        def multiply(bank, i, j, n, pos, gs):
+            cols = slice(P * j, P * (j + n))
+            for g in gs:
+                nc.tensor.matmul_mx(out=bank[:, P * pos:P * (pos + n)], lhsT=a_codes[:, i, g, :].bitcast(FP8X4), lhsT_scale=a_scales[:, i, g, :],
+                                    rhs=l_codes[g][:, cols].bitcast(FP8X4), rhs_scale=l_scales[g][:, cols],
+                                    start=(g == 0), stop=(g == GROUPS - 1))
 
-        def out_step():
-            c, blocks = ready.pop(0)
-            width = P * len(blocks)
-            bank = psum.tile([P, 512], F32, tag="out", name="acc")
-            row = [j for i, j in blocks if i == c]
-            col = [i for i, j in blocks if i != c]
-            runs = []
-            at = 0
-            while row:
-                n = 4 if len(row) == 4 else 2 if len(row) >= 2 else 1
-                runs.append((c, row[0], n, at))
-                row = row[n:]
-                at += n
-            for i in col:
-                runs.append((i, c, 1, at))
-                at += 1
-            for i, j, n, pos in runs:
-                cols = slice(P * j, P * (j + n))
-                for g in range(GROUPS):
-                    nc.tensor.matmul_mx(out=bank[:, P * pos:P * (pos + n)], lhsT=a_codes[:, i, g, :].bitcast(FP8X4), lhsT_scale=a_scales[:, i, g, :],
-                                        rhs=l_codes[g][:, cols].bitcast(FP8X4), rhs_scale=l_scales[g][:, cols],
-                                        start=(g == 0), stop=(g == GROUPS - 1))
-            copies.append((c, blocks, bank, width))
-
-        def copy_out(engine):
-            c, blocks, bank, width = copies.pop(0)
+        def store(bank, i, rows, j, n, engine):
+            width = P * rows * n
             res = stage.tile([P, 512], F32, tag="res", bufs=4, name="res")
             if engine == "scalar":
                 nc.scalar.activation(out=res[:, :width], in_=bank[:, :width], func=COPY, scale=OUT_SCALE)
             else:
                 nc.vector.tensor_scalar(out=res[:, :width], in0=bank[:, :width], scalar1=OUT_SCALE, scalar2=None, op0=MULT)
-            row = [j for i, j in blocks if i == c]
-            col = [i for i, j in blocks if i != c]
-            if row:
-                nc.sync.dma_start(out=out[P * c:P * (c + 1), P * row[0]:P * (row[-1] + 1)], in_=res[:, :P * len(row)])
-            if col:
-                nc.sync.dma_start(out=out_rows[:, col[0]:col[-1] + 1, P * c:P * (c + 1)],
-                                  in_=res[:, P * len(row):width].rearrange("p (i n) -> p i n", n=P))
+            nc.sync.dma_start(out=out_rows[:, i:i + rows, P * j:P * (j + n)], in_=res[:, :width].rearrange("p (i n) -> p i n", i=rows))
 
-        interleave_w(nc.vector.tensor_copy, 0)
-        turn("f", 0, 0)
-        turn("f", 0, 1)
+        def add_row(i, count):
+            for j in range(0, count, 4):
+                ready.append((i, 1, j, min(4, count - j)))
+
+        def add_column(j, n, count):
+            per = 4 // n
+            for i in range(0, count, per):
+                ready.append((i, min(per, count - i), j, n))
+
+        def out_step(tag, engine):
+            i, rows, j, n = ready.pop(0)
+            bank = psum.tile([P, 512], F32, tag=tag, name="acc")
+            for r in range(rows):
+                multiply(bank, i + r, j, n, r * n, range(GROUPS))
+            store(bank, i, rows, j, n, engine)
+
         nc.scalar.copy(out=bias_rows[0:CHUNKS, :], in_=b_rows[:])
+        interleave_w(nc.vector.tensor_copy, 0)
+        widen(0, 0)
+        turn("x", 0, 0)
+        quantize_w(0)
+        widen(0, 1)
+        turn("x", 0, 1)
+        turn("f", 0, 0)
+        widen(1, 0)
+        turn("x", 1, 0)
+        quantize_rows("x", 0)
+        turn("f", 0, 1)
+        widen(1, 1)
+        turn("x", 1, 1)
         b_turn = psum.tile([P, P], F32, tag="zt", name="b_turn")
         nc.tensor.transpose(b_turn[:], bias_rows[:], ident[:])
         b_cols = keep.tile([P, CHUNKS], F32)
         nc.scalar.copy(out=b_cols[:], in_=b_turn[:, 0:CHUNKS])
-        widen(0, 0)
-        widen(0, 1)
-        turn("x", 0, 0)
-        quantize_w(0)
-        widen(0, 2)
-        widen(0, 3)
-        turn("x", 0, 1)
         quantize_rows("f", 0)
-        widen(1, 0)
-        widen(1, 1)
-        turn("x", 1, 0)
-        quantize_rows("x", 0)
-        widen(1, 2)
-        widen(1, 3)
-        turn("x", 1, 1)
         turn("f", 1, 0)
         turn("f", 1, 1)
         widen(2, 0)
+        turn("x", 2, 0)
         quantize_rows("x", 1)
-        widen(2, 1)
-        quantize_rows("f", 1)
         z_step(0)
         tanh_step(0)
         z_step(1)
+        widen(2, 1)
+        turn("x", 2, 1)
         tanh_step(1)
-
+        quantize_rows("f", 1)
         turn_tags.remove("zd")
         turned[0] = 0
+        fill = [lambda: widen(3, 0),
+                lambda: turn("x", 3, 0),
+                lambda: quantize_rows("x", 2),
+                lambda: widen(3, 1),
+                lambda: turn("x", 3, 1),
+                lambda: interleave_w(nc.scalar.copy, 1),
+                lambda: turn("f", 2, 0),
+                lambda: quantize_rows("x", 3),
+                lambda: turn("f", 2, 1),
+                lambda: turn("f", 3, 0),
+                lambda: quantize_w(1),
+                lambda: turn("f", 3, 1),
+                lambda: quantize_rows("f", 2),
+                lambda: quantize_rows("f", 3),
+                lambda: interleave_w(nc.scalar.copy, 2),
+                lambda: quantize_w(2),
+                lambda: interleave_w(nc.scalar.copy, 3),
+                lambda: quantize_w(3)]
 
-        def extra_0():
-            turn("x", 2, 0)
-            widen(2, 2)
-            widen(2, 3)
-            turn("x", 2, 1)
-            widen(3, 0)
-            widen(3, 1)
-            turn("x", 3, 0)
-            quantize_rows("x", 2)
-            widen(3, 2)
-            widen(3, 3)
-            turn("x", 3, 1)
+        def fill_in(n):
+            for step in range(n):
+                if fill:
+                    fill.pop(0)()
 
-        def extra_1():
-            turn("f", 2, 0)
-            turn("f", 2, 1)
-            turn("f", 3, 0)
-            quantize_rows("f", 2)
-            turn("f", 3, 1)
-            quantize_rows("f", 3)
-
+        fill_in(2)
         last = len(PAIRS) - 1
-        for k in range(len(PAIRS)):
+        final = CHUNKS - 1
+
+        def quantize_pair(k):
+            c, h = PAIRS[k]
+            if c < SINGLE:
+                if h == 1:
+                    quantize_a(c, slice(0, GROUPS))
+                    if c >= 2:
+                        add_row(c, c - c % 2)
+                if c % 2 == 1:
+                    for g in groups(k):
+                        quantize_l(c - 1, 2, g)
+                    if h == 1:
+                        add_column(c - 1, 2, c + 1)
+            else:
+                quantize_a(c, slice(2 * h, 2 * h + 2))
+                for g in groups(k):
+                    quantize_l(c, 1, g)
+                if h == 1 and c < final:
+                    add_row(c, c)
+                    add_column(c, 1, c + 1)
+
+        def prepare(k):
             if is_turned(k):
                 turn_psi_step(k)
-                square_step(k)
+            square_step(k)
+
+        prepare(0)
+        zd_step(0)
+        fill_in(4)
+        if True:
+            for k in range(last):
                 a_step(k)
-            if k == 0:
-                zd_step(0)
-                extra_0()
-                quantize_rows("x", 3)
-                z_step(2)
-            elif k + 2 <= last:
-                z_step(k + 2)
-            if is_turned(k) and k > 0:
-                zd_step(k)
-            if is_turned(k + 2):
-                tanh_step(k + 2)
-            if is_turned(k) and k > 0:
-                quantize_l(k - 1)
-            l_step(k)
-            if is_direct(k):
-                quantize_l(k - 1)
-            if is_direct(k + 2):
-                bias_step(k + 2)
-            if is_direct(k + 1):
+                if k == 0:
+                    fill_in(5)
+                prepare(k + 1)
+                fill_in(1)
+                if k + 2 <= last:
+                    z_step(k + 2)
+                    tanh_step(k + 2)
+                if k > 0:
+                    quantize_pair(k - 1)
+                l_step(k)
                 zd_step(k + 1)
-                tanh_step(k + 1)
-                square_step(k + 1)
-                a_step(k + 1)
-            quantize_a(k)
-            if k == 0:
-                extra_1()
-                interleave_w(nc.scalar.copy, 1)
-            if k == 1:
-                quantize_w(1)
-            if k > 0:
-                cp, hp = PAIRS[k - 1]
-                if hp == 1:
-                    add_blocks(cp)
-            for turn_out in range(2 if k < last else 0):
-                if ready:
-                    out_step()
-                    copy_out("scalar")
-        quantize_l(last)
-        while ready:
-            out_step()
-            copy_out("scalar")
-        add_blocks(CHUNKS - 1)
-        order = 0
-        while ready:
-            out_step()
-            copy_out("scalar" if order % 2 else "vector")
-            order += 1
+                fill_in(3)
+                for step in range(2):
+                    if ready:
+                        out_step("out", "scalar")
+                if k == last - 1:
+                    quantize_pair(k)
+            l_step(last)
+            for g in groups(last):
+                quantize_l(final, 1, g)
+            add_column(final, 1, final)
+            a_step(last)
+            quantize_a(final, slice(2, 4))
+            rows = [psum.tile([P, 512], F32, tag="zt", name="row") for j in range(2)]
+            while ready:
+                if len(ready) == 2:
+                    for j in range(2):
+                        multiply(rows[j], final, 4 * j, 4, 0, (0, 1))
+                out_step("out", "scalar")
+            for j in range(2):
+                multiply(rows[j], final, 4 * j, 4, 0, (2, 3))
+            store(rows[0], final, 1, 0, 4, "vector")
+            store(rows[1], final, 1, 4, 4, "scalar")

import math
from contextlib import ExitStack

import concourse.mybir as mybir
from concourse.masks import make_identity

N, D, F = 2048, 512, 1024
FLOPS = 2 * N * D * F * 2 + 2 * N * F * F

F32 = mybir.dt.float32
BF16 = mybir.dt.bfloat16
U32 = mybir.dt.uint32
U8 = mybir.dt.uint8
FP8 = mybir.dt.float8_e4m3fn
FP8X4 = mybir.dt.float8_e4m3fn_x4
ADD = mybir.AluOpType.add
MULT = mybir.AluOpType.mult
COPY = mybir.ActivationFunctionType.Copy
TANH = mybir.ActivationFunctionType.Tanh
SQUARE = mybir.ActivationFunctionType.Square

P = 128
T4 = 4
GROUP = P * T4
GROUPS = N // GROUP
WQ = 256
SINGLE = 6
CHUNKS = F // P
OUT_SCALE = -1.0 / math.sqrt(N)
PAIRS = [(0, 0), (1, 0), (0, 1), (1, 1)] + [(c, h) for c in range(2, CHUNKS) for h in range(2)]
MODES = "TTTTTTTT"


def tile_generatoredmdstiffnessmatrix_kernel(tc, x_bytes, x_scale, f, w, b, q, out):
    nc = tc.nc
    with ExitStack() as ctx:
        keep = ctx.enter_context(tc.tile_pool(name="keep", bufs=1))
        stage = ctx.enter_context(tc.tile_pool(name="stage", bufs=2))
        psum = ctx.enter_context(tc.psum_pool(name="psum", bufs=2))

        scale_rows = keep.tile([P, P], F32)
        nc.vector.memset(scale_rows[:], 0.0)
        warm = keep.tile([P, 1], F32)
        nc.vector.memset(warm[:], 0.0)
        ident = keep.tile([P, P], F32)
        make_identity(nc, ident[:])
        bias_rows = keep.tile([P, P], F32)
        nc.gpsimd.memset(bias_rows[:], 0.0)

        nc.sync.dma_start(out=scale_rows[0:4, :], in_=x_scale.rearrange("o (c n) -> (o c) n", n=P))
        b_rows = keep.tile([CHUNKS, P], BF16)
        nc.scalar.dma_start(out=b_rows[:], in_=b.rearrange("(c m) -> c m", m=P))
        warm_out = keep.tile([P, 1], F32)
        nc.scalar.activation(out=warm_out[:], in_=warm[:], func=TANH)

        w_view = w.rearrange("(p j) c -> p j c", j=T4)
        w_raw = [keep.tile([P, T4, WQ], BF16, name="w_raw%d" % i) for i in range(F // WQ)]
        f_raw = [keep.tile([P, T4, D], BF16, name="f_raw%d" % g) for g in range(GROUPS)]
        x_raw = [keep.tile([P, T4 * D], U8, name="x_raw%d" % g) for g in range(GROUPS)]
        f_view = f.rearrange("(g p t) k -> g p t k", p=P, t=T4)
        x_view = x_bytes.rearrange("(g p t) k -> g p (t k)", p=P, t=T4)

        def load_w(i):
            nc.sync.dma_start(out=w_raw[i][:], in_=w_view[:, :, WQ * i:WQ * (i + 1)])

        def load_f(g):
            nc.sync.dma_start(out=f_raw[g][:], in_=f_view[g])

        def load_x(g):
            nc.sync.dma_start(out=x_raw[g][:], in_=x_view[g])

        q_all = keep.tile([P, GROUPS, T4], BF16)
        load_w(0)
        load_x(0)
        load_f(0)
        load_x(1)
        nc.sync.dma_start(out=q_all[:], in_=q.rearrange("(g p t) -> p g t", p=P, t=T4))
        load_f(1)
        load_x(2)
        load_w(1)
        load_x(3)
        load_f(2)
        load_f(3)
        load_w(2)
        load_w(3)

        s_turn = psum.tile([P, P], F32, tag="zt", name="s_turn")
        nc.tensor.transpose(s_turn[:], scale_rows[:], ident[:])
        s_cols = keep.tile([P, T4], F32)
        nc.scalar.copy(out=s_cols[:], in_=s_turn[:, 0:4])
        s_bank = psum.tile([P, D], F32, tag="zt", name="s_bank")
        for c in range(4):
            nc.tensor.transpose(s_bank[:, P * c:P * (c + 1)], s_cols[:, c:c + 1].to_broadcast([P, P]), ident[:])
        s_all = keep.tile([P, 2, D], F32)
        for i in range(2):
            nc.scalar.copy(out=s_all[:, i, :], in_=s_bank[:])

        w_codes = keep.tile([P, F], U32, align_bytes=64)
        w_scales = keep.tile([P, F], U8, align_bytes=64)
        x_codes = [keep.tile([P, GROUP], U32, align_bytes=64, name="x_codes%d" % g) for g in range(GROUPS)]
        x_scales = [keep.tile([P, GROUP], U8, align_bytes=64, name="x_scales%d" % g) for g in range(GROUPS)]
        f_codes = [keep.tile([P, GROUP], U32, align_bytes=64, name="f_codes%d" % g) for g in range(GROUPS)]
        f_scales = [keep.tile([P, GROUP], U8, align_bytes=64, name="f_scales%d" % g) for g in range(GROUPS)]
        a_codes = keep.tile([P, CHUNKS, GROUPS, P], U32, align_bytes=64)
        a_scales = keep.tile([P, CHUNKS, GROUPS, P], U8, align_bytes=64)
        l_codes = [keep.tile([P, F], U32, align_bytes=64, name="l_codes%d" % g) for g in range(GROUPS)]
        l_scales = [keep.tile([P, F], U8, align_bytes=64, name="l_scales%d" % g) for g in range(GROUPS)]

        def quantize(codes, scales, values):
            nc.vector.quantize_mx(out=codes.bitcast(FP8X4), scales=scales, in_=values)

        w_mx = [keep.tile([P, WQ * T4], BF16, align_bytes=64, name="w_mx%d" % i) for i in range(F // WQ)]

        def interleave_w(engine_copy, i):
            engine_copy(out=w_mx[i][:].rearrange("p (c j) -> p c j", j=T4), in_=w_raw[i][:].rearrange("p j c -> p c j"))

        def quantize_w(i):
            quantize(w_codes[:, WQ * i:WQ * (i + 1)], w_scales[:, WQ * i:WQ * (i + 1)], w_mx[i][:])

        x_vals = {}
        mx_in = {}

        def widen(g, half):
            if half == 0:
                x_vals[g] = stage.tile([P, T4 * D], BF16, tag="x_val", bufs=3, name="x_val%d" % g)
            cols = slice(2 * D * half, 2 * D * (half + 1))
            nc.vector.tensor_tensor(out=x_vals[g][:, cols], in0=x_raw[g][:, cols].bitcast(FP8), in1=s_all[:].rearrange("p i k -> p (i k)"), op=MULT)

        turn_tags = ["ps", "out", "zd"]
        turned = [0]

        def turn(kind, g, half):
            if half == 0:
                mx_in[kind, g] = stage.tile([P, GROUP * T4], BF16, tag="mx_in", bufs=4, align_bytes=64, name="mx_in_%s%d" % (kind, g))
            src = x_vals[g][:] if kind == "x" else f_raw[g][:].rearrange("p t k -> p (t k)")
            words = src.bitcast(F32)
            bank = psum.tile([P, 2, 2, P], F32, tag=turn_tags[turned[0] % len(turn_tags)], name="turn")
            turned[0] += 1
            for s in range(2):
                w0 = 256 * (2 * half + s)
                for u in range(2):
                    nc.tensor.transpose(bank[:, s, u, :], words[:, w0 + u:w0 + 256:2], ident[:])
            dst = mx_in[kind, g][:].bitcast(F32)[:, 512 * half:512 * (half + 1)]
            nc.scalar.copy(out=dst.rearrange("p (s r u) -> p s r u", s=2, u=2), in_=bank[:].rearrange("p s u r -> p s r u"))

        def quantize_rows(kind, g):
            if kind == "x":
                quantize(x_codes[g][:], x_scales[g][:], mx_in[kind, g][:])
            else:
                quantize(f_codes[g][:], f_scales[g][:], mx_in[kind, g][:])

        def w_cols(c):
            cols = slice(P * c, P * (c + 1))
            return w_codes[:, cols].bitcast(FP8X4), w_scales[:, cols]

        live = {}

        def groups(k):
            c, h = PAIRS[k]
            return [2 * h, 2 * h + 1]

        def is_turned(k):
            return 0 <= k < len(PAIRS) and MODES[PAIRS[k][0]] == "T"

        def is_direct(k):
            return 0 <= k < len(PAIRS) and MODES[PAIRS[k][0]] != "T"

        def sample_first(codes, scales, g, c, tag, name):
            bank = psum.tile([P, T4, P], F32, tag=tag, name=name)
            rhs, rhs_scale = w_cols(c)
            for t in range(T4):
                cols = slice(P * t, P * (t + 1))
                nc.tensor.matmul_mx(out=bank[:, t, :], lhsT=codes[g][:, cols].bitcast(FP8X4), lhsT_scale=scales[g][:, cols],
                                    rhs=rhs, rhs_scale=rhs_scale, start=True, stop=True)
            return bank

        def z_step(k):
            c = PAIRS[k][0]
            banks = []
            for g in groups(k):
                if is_turned(k):
                    bank = psum.tile([P, GROUP], F32, tag="zt", name="zt")
                    lhs, lhs_scale = w_cols(c)
                    nc.tensor.matmul_mx(out=bank[:], lhsT=lhs, lhsT_scale=lhs_scale, rhs=x_codes[g][:].bitcast(FP8X4),
                                        rhs_scale=x_scales[g][:], start=True, stop=True)
                else:
                    bank = sample_first(x_codes, x_scales, g, c, "zt", "z")
                banks.append(bank)
            live["z", k] = banks

        def tanh_step(k):
            c = PAIRS[k][0]
            psi = stage.tile([P, 2, GROUP], F32, tag="psi", bufs=4, name="psi")
            for i in range(2):
                if is_turned(k):
                    nc.scalar.activation(out=psi[:, i], in_=live["z", k][i][:], func=TANH, bias=b_cols[:, c:c + 1])
                else:
                    nc.scalar.activation(out=psi[:, i], in_=live["zb", k][:, i].rearrange("p n t -> p (n t)"), func=TANH)
            live["psi", k] = psi

        def turn_psi_step(k):
            banks = []
            for i in range(2):
                bank = psum.tile([P, T4, P], F32, tag="ps", name="ps")
                for t in range(T4):
                    nc.tensor.transpose(bank[:, t, :], live["psi", k][:, i, P * t:P * (t + 1)], ident[:])
                banks.append(bank)
            live["ps", k] = banks

        def square_step(k):
            sq = stage.tile([P, 2, P, T4], F32, tag="sq", bufs=4, name="sq")
            for i in range(2):
                if is_turned(k):
                    nc.scalar.activation(out=sq[:, i], in_=live["ps", k][i][:].rearrange("p t n -> p n t"), func=SQUARE)
                else:
                    nc.scalar.activation(out=sq[:, i].rearrange("p n t -> p (n t)"), in_=live["psi", k][:, i], func=SQUARE)
            live["sq", k] = sq

        def a_step(k):
            c, h = PAIRS[k]
            if h == 0:
                live["a", c] = stage.tile([P, GROUPS, P, T4], BF16, tag="a_mx", bufs=3, align_bytes=64, name="a_mx")
            a_mx = live["a", c]
            for i, g in enumerate(groups(k)):
                weight = q_all[:, g, :].unsqueeze(1).to_broadcast([P, P, T4])
                if is_turned(k):
                    nc.vector.tensor_tensor(out=a_mx[:, g], in0=live["ps", k][i][:].rearrange("p t n -> p n t"), in1=weight, op=MULT)
                elif MODES[PAIRS[k][0]] == "V" or (MODES[PAIRS[k][0]] == "H" and i == 1):
                    nc.vector.tensor_tensor(out=a_mx[:, g], in0=live["psi", k][:, i].rearrange("p (n t) -> p n t", t=T4), in1=weight, op=MULT)
                else:
                    nc.gpsimd.tensor_tensor(out=a_mx[:, g], in0=live["psi", k][:, i].rearrange("p (n t) -> p n t", t=T4), in1=weight, op=MULT)

        def zd_step(k):
            live["zd", k] = [sample_first(f_codes, f_scales, g, PAIRS[k][0], "zd", "zd") for g in groups(k)]

        def l_step(k):
            c, h = PAIRS[k]
            if h == 0 and (c % 2 == 0 or c >= SINGLE):
                live["l", c] = stage.tile([P, GROUPS, 2, P, T4], BF16, tag="l_mx", bufs=2, align_bytes=64, name="l_mx")
                if c < SINGLE:
                    live["l", c + 1] = live["l", c]
            at = 0 if c >= SINGLE else c % 2
            for i, g in enumerate(groups(k)):
                nc.vector.scalar_tensor_tensor(out=live["l", c][:, g, at], in0=live["sq", k][:, i], scalar=-1.0,
                                               in1=live["zd", k][i][:].rearrange("p t n -> p n t"), op0=ADD, op1=MULT)

        def quantize_a(c, gs):
            quantize(a_codes[:, c, gs, :].rearrange("p g n -> p (g n)"), a_scales[:, c, gs, :].rearrange("p g n -> p (g n)"),
                     live["a", c][:, gs].rearrange("p g n t -> p (g n t)"))

        def quantize_l(c, width, g):
            cols = slice(P * c, P * (c + width))
            quantize(l_codes[g][:, cols], l_scales[g][:, cols], live["l", c][:, g, 0:width].rearrange("p c n t -> p (c n t)"))

        out_rows = out.rearrange("(i p) n -> p i n", p=P)
        ready = []

        def multiply(bank, i, j, n, pos, gs):
            cols = slice(P * j, P * (j + n))
            for g in gs:
                nc.tensor.matmul_mx(out=bank[:, P * pos:P * (pos + n)], lhsT=a_codes[:, i, g, :].bitcast(FP8X4), lhsT_scale=a_scales[:, i, g, :],
                                    rhs=l_codes[g][:, cols].bitcast(FP8X4), rhs_scale=l_scales[g][:, cols],
                                    start=(g == 0), stop=(g == GROUPS - 1))

        def store(bank, i, rows, j, n, engine):
            width = P * rows * n
            res = stage.tile([P, 512], F32, tag="res", bufs=4, name="res")
            if engine == "scalar":
                nc.scalar.activation(out=res[:, :width], in_=bank[:, :width], func=COPY, scale=OUT_SCALE)
            else:
                nc.vector.tensor_scalar(out=res[:, :width], in0=bank[:, :width], scalar1=OUT_SCALE, scalar2=None, op0=MULT)
            nc.sync.dma_start(out=out_rows[:, i:i + rows, P * j:P * (j + n)], in_=res[:, :width].rearrange("p (i n) -> p i n", i=rows))

        def add_row(i, count):
            for j in range(0, count, 4):
                ready.append((i, 1, j, min(4, count - j)))

        def add_column(j, n, count):
            per = 4 // n
            for i in range(0, count, per):
                ready.append((i, min(per, count - i), j, n))

        def out_step(tag, engine):
            i, rows, j, n = ready.pop(0)
            bank = psum.tile([P, 512], F32, tag=tag, name="acc")
            for r in range(rows):
                multiply(bank, i + r, j, n, r * n, range(GROUPS))
            store(bank, i, rows, j, n, engine)

        nc.scalar.copy(out=bias_rows[0:CHUNKS, :], in_=b_rows[:])
        interleave_w(nc.vector.tensor_copy, 0)
        widen(0, 0)
        turn("x", 0, 0)
        quantize_w(0)
        widen(0, 1)
        turn("x", 0, 1)
        turn("f", 0, 0)
        widen(1, 0)
        turn("x", 1, 0)
        quantize_rows("x", 0)
        turn("f", 0, 1)
        widen(1, 1)
        turn("x", 1, 1)
        b_turn = psum.tile([P, P], F32, tag="zt", name="b_turn")
        nc.tensor.transpose(b_turn[:], bias_rows[:], ident[:])
        b_cols = keep.tile([P, CHUNKS], F32)
        nc.scalar.copy(out=b_cols[:], in_=b_turn[:, 0:CHUNKS])
        quantize_rows("f", 0)
        turn("f", 1, 0)
        turn("f", 1, 1)
        widen(2, 0)
        turn("x", 2, 0)
        quantize_rows("x", 1)
        z_step(0)
        tanh_step(0)
        z_step(1)
        widen(2, 1)
        turn("x", 2, 1)
        tanh_step(1)
        quantize_rows("f", 1)
        turn_tags.remove("zd")
        turned[0] = 0
        fill = [lambda: widen(3, 0),
                lambda: turn("x", 3, 0),
                lambda: quantize_rows("x", 2),
                lambda: widen(3, 1),
                lambda: turn("x", 3, 1),
                lambda: interleave_w(nc.scalar.copy, 1),
                lambda: turn("f", 2, 0),
                lambda: quantize_rows("x", 3),
                lambda: turn("f", 2, 1),
                lambda: turn("f", 3, 0),
                lambda: quantize_w(1),
                lambda: turn("f", 3, 1),
                lambda: quantize_rows("f", 2),
                lambda: quantize_rows("f", 3),
                lambda: interleave_w(nc.scalar.copy, 2),
                lambda: quantize_w(2),
                lambda: interleave_w(nc.scalar.copy, 3),
                lambda: quantize_w(3)]

        def fill_in(n):
            for step in range(n):
                if fill:
                    fill.pop(0)()

        fill_in(2)
        last = len(PAIRS) - 1
        final = CHUNKS - 1

        def quantize_pair(k):
            c, h = PAIRS[k]
            if c < SINGLE:
                if h == 1:
                    quantize_a(c, slice(0, GROUPS))
                    if c >= 2:
                        add_row(c, c - c % 2)
                if c % 2 == 1:
                    for g in groups(k):
                        quantize_l(c - 1, 2, g)
                    if h == 1:
                        add_column(c - 1, 2, c + 1)
            else:
                quantize_a(c, slice(2 * h, 2 * h + 2))
                for g in groups(k):
                    quantize_l(c, 1, g)
                if h == 1 and c < final:
                    add_row(c, c)
                    add_column(c, 1, c + 1)

        def prepare(k):
            if is_turned(k):
                turn_psi_step(k)
            square_step(k)

        prepare(0)
        zd_step(0)
        fill_in(4)
        if True:
            for k in range(last):
                a_step(k)
                if k == 0:
                    fill_in(5)
                prepare(k + 1)
                fill_in(1)
                if k + 2 <= last:
                    z_step(k + 2)
                    tanh_step(k + 2)
                if k > 0:
                    quantize_pair(k - 1)
                l_step(k)
                zd_step(k + 1)
                fill_in(3)
                for step in range(2):
                    if ready:
                        out_step("out", "scalar")
                if k == last - 1:
                    quantize_pair(k)
            l_step(last)
            for g in groups(last):
                quantize_l(final, 1, g)
            add_column(final, 1, final)
            a_step(last)
            quantize_a(final, slice(2, 4))
            rows = [psum.tile([P, 512], F32, tag="zt", name="row") for j in range(2)]
            while ready:
                if len(ready) == 2:
                    for j in range(2):
                        multiply(rows[j], final, 4 * j, 4, 0, (0, 1))
                out_step("out", "scalar")
            for j in range(2):
                multiply(rows[j], final, 4 * j, 4, 0, (2, 3))
            store(rows[0], final, 1, 0, 4, "vector")
            store(rows[1], final, 1, 4, 4, "scalar")
